import numpy as np
import ml_dtypes


def mxq(x, axis, fmt="e4m3"):
    dtype, down = {"e4m3": (ml_dtypes.float8_e4m3fn, 7), "e5m2": (ml_dtypes.float8_e5m2, 14)}[fmt]
    v = np.moveaxis(np.asarray(x, np.float32).astype(ml_dtypes.bfloat16).astype(np.float64), axis, -1)
    blocks = v.reshape(v.shape[:-1] + (-1, 32))
    amax = np.abs(blocks).max(-1, keepdims=True)
    byte = np.maximum(np.where(amax > 0, np.frexp(amax)[1] - 1 + 127, 0) - down, 1)
    scale = np.exp2(byte - 127.0)
    codes = (blocks / scale).astype(np.float32).astype(dtype).astype(np.float64)
    return np.moveaxis((codes * scale).reshape(v.shape), -1, axis)


WIDE = False


def mx_kscale(k):
    if not WIDE:
        return np.ones(k)
    levels = np.array([10, -10, 5, -5, 0])
    if k % 512:
        return np.exp2(np.random.permutation(np.resize(levels, k // 32))).repeat(32)
    a = np.empty((k // 512, 16))
    for p in range(k // 512):
        a[p, :8] = np.random.permutation(np.resize(levels, 8))
        for g in range(8):
            far = levels[np.abs(levels - a[p, g]) >= 10]
            a[p, g + 8] = far[np.random.randint(len(far))]
    return np.exp2(a.ravel()).repeat(32)


def f64(x):
    return np.asarray(x).astype(np.float64)


def striped(idx):
    return np.tile(np.asarray(idx).reshape(-1, 16).T, (8, 1)).astype(np.uint16)


def unstriped(offs):
    return offs[:16].T.reshape(-1).astype(np.int64)


def striped8(idx):
    return np.asarray(idx).reshape(8, -1, 16).transpose(0, 2, 1).reshape(128, -1).astype(np.uint16)


def unstriped8(offs):
    return offs.reshape(8, 16, -1).transpose(0, 2, 1).reshape(8, -1).astype(np.int64)


def pick8(x, idx, run):
    r = np.arange(len(x))
    return x[r[:, None], idx[r % (8 * run) // run]]


E2M1 = np.array([0.0, 0.5, 1.0, 1.5, 2.0, 3.0, 4.0, 6.0, -0.0, -0.5, -1.0, -1.5, -2.0, -3.0, -4.0, -6.0])


def pack_weight(w, fmt):
    k, n = w.shape
    w = f64(np.asarray(w, np.float32).astype(ml_dtypes.bfloat16)).reshape(k // 32, 32, n)
    amax = np.abs(w).max(1)
    if fmt == "e4m3":
        byte = np.frexp(amax)[1] - 1 + 127 - 7
    else:
        mant, ex = np.frexp(amax / 6.0)
        byte = np.where(mant > 0.5, ex, ex - 1) + 127
    byte = np.clip(np.where(amax > 0, byte, 1), 1, 254)
    scaled = (w * np.exp2(127.0 - byte)[:, None, :]).reshape(k, n).astype(np.float32)
    by_word = np.ascontiguousarray(scaled.reshape(k // 512, 128, 4, n).transpose(0, 1, 3, 2))
    if fmt == "e4m3":
        words = by_word.astype(ml_dtypes.float8_e4m3fn).view(np.uint8)
    else:
        c = by_word.astype(ml_dtypes.float4_e2m1fn).view(np.uint8) & 0xF
        words = (c[..., 0::2] | (c[..., 1::2] << 4)).reshape(k // 512, 128, 2 * n)
    return np.ascontiguousarray(words), np.ascontiguousarray(byte.astype(np.uint8).reshape(k // 512, 16, n))


def unpack_weight(words, scales, fmt):
    g, _, n = scales.shape
    words = np.ascontiguousarray(words).reshape(g, 128, n, -1)
    if fmt == "e4m3":
        vals = words.view(ml_dtypes.float8_e4m3fn).astype(np.float64)
    else:
        nib = np.empty((g, 128, n, 4), np.uint8)
        nib[..., 0::2] = words & 0xF
        nib[..., 1::2] = words >> 4
        vals = E2M1[nib]
    vals = vals * np.repeat(np.exp2(scales.astype(np.float64) - 127.0), 8, axis=1)[..., None]
    return vals.transpose(0, 1, 3, 2).reshape(g * 512, n)


K, J, R, T, F, G, O, C, N, S = 512, 512, 512, 1024, 1024, 384, 256, 1024, 256, 1024


def setup_inputs():
    n = np.random.standard_normal
    idx = np.random.permutation(T)[:J]
    idx2 = np.stack([np.random.permutation(F)[:G] for _ in range(8)])
    idx3 = np.stack([np.random.permutation(R)[:G] for _ in range(8)])
    idx4 = np.stack([np.random.permutation(C)[:J] for _ in range(8)])
    idx5 = np.stack([np.random.permutation(C)[:O] for _ in range(8)])
    idx6 = np.stack([np.random.permutation(C)[:O] for _ in range(8)])
    idx7 = np.random.permutation(S)[:N]
    fk = mx_kscale(K)
    fr = mx_kscale(R)
    xtp = pack_weight(n((K, T)) * fk[:, None], "e4m3")
    vsp = pack_weight(n((R, S)) * 1 / np.sqrt(R) / fr[:, None], "e4m3")
    return {
        "xt_words": xtp[0],
        "xt_scales": xtp[1],
        "ua": (np.random.randint(-7, 8, (K, F)).astype(np.float64)).astype(np.float32),
        "ha": ((np.random.randint(8, 25, (K, 1)) / 1024.0) / fk[:, None]).astype(np.float32),
        "sa": (np.random.uniform(0.5, 1.6, (R, 1)) * fr[:, None]).astype(np.float32),
        "sb": (np.random.uniform(0.5, 1.6, (R, 1)) * fr[:, None]).astype(np.float32),
        "vs_words": vsp[0],
        "vs_scales": vsp[1],
        "offs": striped(idx),
        "offs2": striped8(idx2),
        "offs3": striped8(idx3),
        "offs4": striped8(idx4),
        "offs5": striped8(idx5),
        "offs6": striped8(idx6),
        "offs7": striped(idx7),
    }


def reference(xt_words, xt_scales, ua, ha, sa, sb, vs_words, vs_scales, offs, offs2, offs3, offs4, offs5, offs6, offs7):
    idx = unstriped(offs)
    idx2 = unstriped8(offs2)
    idx3 = unstriped8(offs3)
    idx4 = unstriped8(offs4)
    idx5 = unstriped8(offs5)
    idx6 = unstriped8(offs6)
    idx7 = unstriped(offs7)
    xtu = unpack_weight(xt_words, xt_scales, "e4m3")
    vsu = unpack_weight(vs_words, vs_scales, "e4m3")
    wcd = pick8(f64(ua), idx2, 64) * f64(ha)
    wc = np.zeros((K, R))
    wc[np.arange(K)[:, None], idx3[np.arange(K) % 512 // 64]] = wcd
    wcq = mxq(wc, 0, "e4m3")
    xtidxg = xtu[:, idx]
    a = wcq.T @ xtidxg
    pw = np.zeros((R, C))
    pw[np.arange(R)[:, None], idx4[np.arange(R) % 512 // 64]] = a
    hid = np.maximum(pick8(pw, idx5, 64) * f64(sa), pick8(pw, idx6, 64) * f64(sb))
    vsidx7g = vsu[:, idx7]
    hidq = mxq(hid, 0, "e4m3")
    y = vsidx7g.T @ hidq
    return y

@@ -1,0 +1,181 @@
+from contextlib import ExitStack
+
+import concourse.mybir as mybir
+
+K, J, R, T, F, G, O, C, N, S = 512, 512, 512, 1024, 1024, 384, 256, 1024, 256, 1024
+FLOPS = 2 * K * R * J + 2 * R * N * O
+
+F32 = mybir.dt.float32
+BF16 = mybir.dt.bfloat16
+I32 = mybir.dt.int32
+U32 = mybir.dt.uint32
+U16 = mybir.dt.uint16
+U8 = mybir.dt.uint8
+FP8X4 = mybir.dt.float8_e4m3fn_x4
+COPY = mybir.ActivationFunctionType.Copy
+MAX = mybir.AluOpType.max
+
+P = 128
+PACK = 4
+FIRST = 128
+
+
+def tile_picked_tokens_sparsecodes_one_boardpair_store_plain_kernel(
+    tc, xt_words, xt_scales, ua, ha, sa, sb, vs_words, vs_scales, offs, offs2, offs3, offs4, offs5, offs6, offs7, out
+):
+    nc = tc.nc
+    with ExitStack() as ctx:
+        keep = ctx.enter_context(tc.tile_pool(name="keep", bufs=1))
+        psum = ctx.enter_context(tc.psum_pool(name="psum", bufs=1))
+
+        def sbuf(name, shape, dtype):
+            return keep.tile(shape, dtype, name=name, align_bytes=64)
+
+        def load_list(name, source):
+            tile = sbuf(name, list(source.shape), U16)
+            nc.sync.dma_start(tile[:], source)
+            return tile
+
+        def load_words(name, source):
+            tile = sbuf(name, [P, source.shape[2]], I32)
+            nc.sync.dma_start(tile[:], source[0].rearrange("p c t -> p (c t)").bitcast(I32))
+            return tile
+
+        def load_scale_rows(tile, source):
+            for q in range(4):
+                nc.sync.dma_start(tile[32 * q : 32 * q + 4, :].bitcast(I32), source[0, 4 * q : 4 * q + 4, :].bitcast(I32))
+
+        def load_factor(name, source, engine):
+            tile = sbuf(name, [P, PACK], F32)
+            engine.dma_start(tile[:], source.rearrange("(p t) one -> p (t one)", t=PACK))
+            return tile
+
+        xt_scale_table = sbuf("xt_scale_table", [P, T], U8)
+        vs_scale_table = sbuf("vs_scale_table", [P, S], U8)
+        wc = [sbuf("wc%d" % t, [P, R], F32) for t in range(PACK)]
+        board = [sbuf("board%d" % t, [P, C], F32) for t in range(PACK)]
+        nc.vector.memset(xt_scale_table[:].bitcast(I32), 0)
+        nc.vector.memset(vs_scale_table[:].bitcast(I32), 0)
+        for t in range(PACK):
+            nc.vector.memset(wc[t][:], 0.0)
+
+        ua_rows = ua.rearrange("(p t) f -> p t f", t=PACK)
+        ua_table = [sbuf("ua_table%d" % t, [P, F], F32) for t in range(PACK)]
+        nc.sync.dma_start(ua_table[0][:], ua_rows[:, 0, :])
+        step = load_factor("step", ha, nc.scalar)
+        code_list = load_list("code_list", offs2)
+        fill_list = load_list("fill_list", offs3)
+        for t in range(1, PACK):
+            nc.sync.dma_start(ua_table[t][:], ua_rows[:, t, :])
+        token_list = load_list("token_list", offs)
+        xt_word_table = load_words("xt_word_table", xt_words)
+        load_scale_rows(xt_scale_table, xt_scales)
+        put_list = load_list("put_list", offs4)
+        first_list = load_list("first_list", offs5)
+        second_list = load_list("second_list", offs6)
+        first_weight = load_factor("first_weight", sa, nc.sync)
+        second_weight = load_factor("second_weight", sb, nc.sync)
+        store_list = load_list("store_list", offs7)
+        vs_word_table = load_words("vs_word_table", vs_words)
+        load_scale_rows(vs_scale_table, vs_scales)
+
+        for t in range(PACK):
+            nc.vector.memset(board[t][:], 0.0)
+
+        xt_codes = sbuf("xt_codes", [P, J], U32)
+        xt_bytes = sbuf("xt_bytes", [P, J], U8)
+        vs_codes = sbuf("vs_codes", [P, N], U32)
+        vs_bytes = sbuf("vs_bytes", [P, N], U8)
+
+        wc_woven = [sbuf("wc_woven%d" % u, [P, P, PACK], BF16) for u in range(PACK)]
+        wc_codes = [sbuf("wc_codes%d" % u, [P, P], U32) for u in range(PACK)]
+        wc_bytes = [sbuf("wc_bytes%d" % u, [P, P], U8) for u in range(PACK)]
+
+        def weave_wc(t, u):
+            nc.vector.tensor_copy(out=wc_woven[u][:, :, t], in_=wc[t][:].rearrange("p (m u) -> p m u", u=PACK)[:, :, u])
+
+        for t in range(PACK):
+            wcd = sbuf("wcd%d" % t, [P, G], F32)
+            nc.scalar.activation(out=wcd[:], in_=ua_table[t][:].indirect(code_list[:]), func=COPY, scale=step[:, t : t + 1])
+            nc.scalar.activation(out=wc[t][:].indirect(fill_list[:]), in_=wcd[:], func=COPY)
+            if t == 1:
+                nc.vector.tensor_copy(out=xt_codes[:], in_=xt_word_table[:].bitcast(U32).indirect(token_list[:]))
+                nc.vector.tensor_copy(out=xt_bytes[:], in_=xt_scale_table[:].indirect(token_list[:]))
+            if t == 2:
+                nc.vector.tensor_copy(out=vs_codes[:], in_=vs_word_table[:].bitcast(U32).indirect(store_list[:]))
+                nc.vector.tensor_copy(out=vs_bytes[:], in_=vs_scale_table[:].indirect(store_list[:]))
+            if t < PACK - 1:
+                for u in range(PACK):
+                    weave_wc(t, u)
+
+        def first_product(u, bank, bank_col, j0, j1):
+            nc.tensor.matmul_mx(
+                out=bank[:, bank_col : bank_col + j1 - j0],
+                lhsT=wc_codes[u][:].bitcast(FP8X4),
+                lhsT_scale=wc_bytes[u][:],
+                rhs=xt_codes[:, j0:j1].bitcast(FP8X4),
+                rhs_scale=xt_bytes[:, j0:j1],
+                start=True,
+                stop=True,
+            )
+
+        def put(u, values, j0, j1):
+            nc.scalar.activation(out=board[u][:].indirect(put_list[:, j0 // 16 : j1 // 16]), in_=values, func=COPY)
+
+        hid_woven = sbuf("hid_woven", [P, O, PACK], BF16)
+
+        def read_board(u):
+            first = sbuf("first%d" % u, [P, O], F32)
+            second = sbuf("second%d" % u, [P, O], F32)
+            nc.scalar.activation(out=first[:], in_=board[u][:].indirect(first_list[:]), func=COPY, scale=first_weight[:, u : u + 1])
+            nc.scalar.activation(out=second[:], in_=board[u][:].indirect(second_list[:]), func=COPY, scale=second_weight[:, u : u + 1])
+            nc.vector.tensor_tensor(out=hid_woven[:, :, u], in0=first[:], in1=second[:], op=MAX)
+
+        for u in range(PACK):
+            weave_wc(PACK - 1, u)
+            nc.vector.quantize_mx(
+                out=wc_codes[u][:].bitcast(FP8X4), scales=wc_bytes[u][:], in_=wc_woven[u][:].rearrange("p m t -> p (m t)")
+            )
+            if u == 0:
+                head_bank = psum.tile([P, FIRST], F32, name="head_bank")
+                rest_bank = psum.tile([P, J - FIRST], F32, name="rest_bank")
+                head = sbuf("a_head", [P, FIRST], F32)
+                rest = sbuf("a_rest", [P, J - FIRST], F32)
+                first_product(0, head_bank, 0, 0, FIRST)
+                first_product(0, rest_bank, 0, FIRST, 2 * FIRST)
+                first_product(0, rest_bank, FIRST, 2 * FIRST, J)
+                nc.scalar.copy(out=head[:], in_=head_bank[:])
+                nc.vector.tensor_copy(out=rest[:], in_=rest_bank[:])
+                put(0, head[:], 0, FIRST)
+                put(0, rest[:], FIRST, J)
+            else:
+                bank = psum.tile([P, J], F32, name="a_bank%d" % u)
+                hidden = sbuf("a%d" % u, [P, J], F32)
+                first_product(u, bank, 0, 0, J)
+                nc.vector.tensor_copy(out=hidden[:], in_=bank[:])
+                put(u, hidden[:], 0, J)
+                read_board(u - 1)
+        read_board(PACK - 1)
+
+        hid_codes = sbuf("hid_codes", [P, O], U32)
+        hid_bytes = sbuf("hid_bytes", [P, O], U8)
+        nc.vector.quantize_mx(out=hid_codes[:].bitcast(FP8X4), scales=hid_bytes[:], in_=hid_woven[:].rearrange("p o t -> p (o t)"))
+        for half in range(N // P):
+            rows = slice(half * P, (half + 1) * P)
+            bank = psum.tile([P, O], F32, name="y_bank%d" % half)
+            result = sbuf("y%d" % half, [P, O], F32)
+            nc.tensor.matmul_mx(
+                out=bank[:],
+                lhsT=vs_codes[:, rows].bitcast(FP8X4),
+                lhsT_scale=vs_bytes[:, rows],
+                rhs=hid_codes[:].bitcast(FP8X4),
+                rhs_scale=hid_bytes[:],
+                start=True,
+                stop=True,
+            )
+            if half == 0:
+                nc.scalar.copy(out=result[:], in_=bank[:])
+                nc.scalar.dma_start(out[rows, :], result[:])
+            else:
+                nc.vector.tensor_copy(out=result[:], in_=bank[:])
+                nc.sync.dma_start(out[rows, :], result[:])

@@ -18,6 +18,7 @@ MAX = mybir.AluOpType.max
 P = 128
 PACK = 4
 FIRST = 128
+HALF = O // 2
 
 
 def tile_picked_tokens_sparsecodes_one_boardpair_store_plain_kernel(
@@ -26,18 +27,18 @@ def tile_picked_tokens_sparsecodes_one_boardpair_store_plain_kernel(
     nc = tc.nc
     with ExitStack() as ctx:
         keep = ctx.enter_context(tc.tile_pool(name="keep", bufs=1))
+        reused = ctx.enter_context(tc.tile_pool(name="reused", bufs=1))
         psum = ctx.enter_context(tc.psum_pool(name="psum", bufs=1))
 
-        def sbuf(name, shape, dtype):
-            return keep.tile(shape, dtype, name=name, align_bytes=64)
+        def sbuf(name, shape, dtype, tag=None):
+            return keep.tile(shape, dtype, name=name, tag=tag or name, align_bytes=64)
 
         def load_list(name, source):
             tile = sbuf(name, list(source.shape), U16)
             nc.sync.dma_start(tile[:], source)
             return tile
 
-        def load_words(name, source):
-            tile = sbuf(name, [P, source.shape[2]], I32)
+        def load_words(tile, source):
             nc.sync.dma_start(tile[:], source[0].rearrange("p c t -> p (c t)").bitcast(I32))
             return tile
 
@@ -52,11 +53,14 @@ def tile_picked_tokens_sparsecodes_one_boardpair_store_plain_kernel(
 
         xt_scale_table = sbuf("xt_scale_table", [P, T], U8)
         vs_scale_table = sbuf("vs_scale_table", [P, S], U8)
-        wc = [sbuf("wc%d" % t, [P, R], F32) for t in range(PACK)]
+        wc = {t: sbuf("wc%d" % t, [P, R], F32) for t in (0, 3)}
         board = [sbuf("board%d" % t, [P, C], F32) for t in range(PACK)]
+        warm = sbuf("warm", [P, 16], F32)
+        nc.vector.memset(warm[:, 0:8], 0.0)
+        nc.scalar.activation(out=warm[:, 8:9], in_=warm[:, 0:1], func=COPY)
         nc.vector.memset(xt_scale_table[:].bitcast(I32), 0)
         nc.vector.memset(vs_scale_table[:].bitcast(I32), 0)
-        for t in range(PACK):
+        for t in wc:
             nc.vector.memset(wc[t][:], 0.0)
 
         ua_rows = ua.rearrange("(p t) f -> p t f", t=PACK)
@@ -65,19 +69,18 @@ def tile_picked_tokens_sparsecodes_one_boardpair_store_plain_kernel(
         step = load_factor("step", ha, nc.scalar)
         code_list = load_list("code_list", offs2)
         fill_list = load_list("fill_list", offs3)
-        for t in range(1, PACK):
-            nc.sync.dma_start(ua_table[t][:], ua_rows[:, t, :])
+        nc.sync.dma_start(ua_table[1][:], ua_rows[:, 1, :])
+        nc.sync.dma_start(ua_table[2][:], ua_rows[:, 2, :])
+        nc.sync.dma_start(ua_table[3][:], ua_rows[:, 3, :])
+        store_list = load_list("store_list", offs7)
+        load_scale_rows(vs_scale_table, vs_scales)
+        vs_word_table = load_words(sbuf("vs_word_table", [P, S], I32), vs_words)
         token_list = load_list("token_list", offs)
-        xt_word_table = load_words("xt_word_table", xt_words)
         load_scale_rows(xt_scale_table, xt_scales)
+        xt_word_table = load_words(reused.tile([P, T], I32, name="xt_word_table", align_bytes=64, offset=0), xt_words)
         put_list = load_list("put_list", offs4)
         first_list = load_list("first_list", offs5)
         second_list = load_list("second_list", offs6)
-        first_weight = load_factor("first_weight", sa, nc.sync)
-        second_weight = load_factor("second_weight", sb, nc.sync)
-        store_list = load_list("store_list", offs7)
-        vs_word_table = load_words("vs_word_table", vs_words)
-        load_scale_rows(vs_scale_table, vs_scales)
 
         for t in range(PACK):
             nc.vector.memset(board[t][:], 0.0)
@@ -87,26 +90,34 @@ def tile_picked_tokens_sparsecodes_one_boardpair_store_plain_kernel(
         vs_codes = sbuf("vs_codes", [P, N], U32)
         vs_bytes = sbuf("vs_bytes", [P, N], U8)
 
-        wc_woven = [sbuf("wc_woven%d" % u, [P, P, PACK], BF16) for u in range(PACK)]
+        nc.vector.tensor_copy(out=vs_bytes[:], in_=vs_scale_table[:].indirect(store_list[:]))
+        nc.vector.tensor_copy(out=vs_codes[:], in_=vs_word_table[:].bitcast(U32).indirect(store_list[:]))
+        nc.vector.tensor_copy(out=xt_bytes[:], in_=xt_scale_table[:].indirect(token_list[:]))
+        nc.vector.tensor_copy(out=xt_codes[:], in_=xt_word_table[:].bitcast(U32).indirect(token_list[:]))
+
         wc_codes = [sbuf("wc_codes%d" % u, [P, P], U32) for u in range(PACK)]
         wc_bytes = [sbuf("wc_bytes%d" % u, [P, P], U8) for u in range(PACK)]
+        woven_tags = [0, 1]
 
-        def weave_wc(t, u):
-            nc.vector.tensor_copy(out=wc_woven[u][:, :, t], in_=wc[t][:].rearrange("p (m u) -> p m u", u=PACK)[:, :, u])
+        def woven_tile(u):
+            if u < 2:
+                return reused.tile([P, P, PACK], BF16, name="wc_woven%d" % u, align_bytes=64, offset=u * 1024)
+            return sbuf("wc_woven%d" % u, [P, P, PACK], BF16, tag="wc_codes%d" % (u - 1))
 
+        def weave_wc(woven, t, u):
+            nc.vector.tensor_copy(out=woven[:, :, t], in_=wc[t][:].rearrange("p (m u) -> p m u", u=PACK)[:, :, u])
+
+        early = [woven_tile(u) for u in range(len(woven_tags))]
         for t in range(PACK):
             wcd = sbuf("wcd%d" % t, [P, G], F32)
             nc.scalar.activation(out=wcd[:], in_=ua_table[t][:].indirect(code_list[:]), func=COPY, scale=step[:, t : t + 1])
+            if t not in wc:
+                wc[t] = sbuf("wc%d" % t, [P, R], F32, tag="ua_table%d" % t)
+                nc.vector.memset(wc[t][:], 0.0)
             nc.scalar.activation(out=wc[t][:].indirect(fill_list[:]), in_=wcd[:], func=COPY)
-            if t == 1:
-                nc.vector.tensor_copy(out=xt_codes[:], in_=xt_word_table[:].bitcast(U32).indirect(token_list[:]))
-                nc.vector.tensor_copy(out=xt_bytes[:], in_=xt_scale_table[:].indirect(token_list[:]))
-            if t == 2:
-                nc.vector.tensor_copy(out=vs_codes[:], in_=vs_word_table[:].bitcast(U32).indirect(store_list[:]))
-                nc.vector.tensor_copy(out=vs_bytes[:], in_=vs_scale_table[:].indirect(store_list[:]))
             if t < PACK - 1:
-                for u in range(PACK):
-                    weave_wc(t, u)
+                for u, woven in enumerate(early):
+                    weave_wc(woven, t, u)
 
         def first_product(u, bank, bank_col, j0, j1):
             nc.tensor.matmul_mx(
@@ -122,19 +133,25 @@ def tile_picked_tokens_sparsecodes_one_boardpair_store_plain_kernel(
         def put(u, values, j0, j1):
             nc.scalar.activation(out=board[u][:].indirect(put_list[:, j0 // 16 : j1 // 16]), in_=values, func=COPY)
 
-        hid_woven = sbuf("hid_woven", [P, O, PACK], BF16)
+        pairs = []
 
         def read_board(u):
             first = sbuf("first%d" % u, [P, O], F32)
             second = sbuf("second%d" % u, [P, O], F32)
             nc.scalar.activation(out=first[:], in_=board[u][:].indirect(first_list[:]), func=COPY, scale=first_weight[:, u : u + 1])
             nc.scalar.activation(out=second[:], in_=board[u][:].indirect(second_list[:]), func=COPY, scale=second_weight[:, u : u + 1])
-            nc.vector.tensor_tensor(out=hid_woven[:, :, u], in0=first[:], in1=second[:], op=MAX)
+            pairs.append((first, second))
 
         for u in range(PACK):
-            weave_wc(PACK - 1, u)
+            if u < len(early):
+                woven = early[u]
+                weave_wc(woven, PACK - 1, u)
+            else:
+                woven = woven_tile(u)
+                for t in range(PACK):
+                    weave_wc(woven, t, u)
             nc.vector.quantize_mx(
-                out=wc_codes[u][:].bitcast(FP8X4), scales=wc_bytes[u][:], in_=wc_woven[u][:].rearrange("p m t -> p (m t)")
+                out=wc_codes[u][:].bitcast(FP8X4), scales=wc_bytes[u][:], in_=woven[:].rearrange("p m t -> p (m t)")
             )
             if u == 0:
                 head_bank = psum.tile([P, FIRST], F32, name="head_bank")
@@ -154,28 +171,54 @@ def tile_picked_tokens_sparsecodes_one_boardpair_store_plain_kernel(
                 first_product(u, bank, 0, 0, J)
                 nc.vector.tensor_copy(out=hidden[:], in_=bank[:])
                 put(u, hidden[:], 0, J)
-                read_board(u - 1)
-        read_board(PACK - 1)
 
-        hid_codes = sbuf("hid_codes", [P, O], U32)
-        hid_bytes = sbuf("hid_bytes", [P, O], U8)
-        nc.vector.quantize_mx(out=hid_codes[:].bitcast(FP8X4), scales=hid_bytes[:], in_=hid_woven[:].rearrange("p o t -> p (o t)"))
-        for half in range(N // P):
-            rows = slice(half * P, (half + 1) * P)
-            bank = psum.tile([P, O], F32, name="y_bank%d" % half)
-            result = sbuf("y%d" % half, [P, O], F32)
+        weights = sbuf("weights", [P, 2, 2 * PACK], F32, tag="wc_bytes1")
+        first_weight = weights[:, 0, :]
+        second_weight = weights[:, 1, :]
+        nc.sync.dma_start(first_weight[:, 0:PACK], sa.rearrange("(p t) one -> p (t one)", t=PACK))
+        nc.sync.dma_start(second_weight[:, 0:PACK], sb.rearrange("(p t) one -> p (t one)", t=PACK))
+        for u in range(PACK):
+            read_board(u)
+
+        hid_woven = [sbuf("hid_woven%d" % h, [P, HALF, PACK], BF16, tag=["wc_codes3", "wc_bytes3"][h]) for h in range(2)]
+        for u, (first, second) in enumerate(pairs):
+            for h in range(2):
+                places = slice(h * HALF, (h + 1) * HALF)
+                nc.vector.tensor_tensor(out=hid_woven[h][:, :, u], in0=first[:, places], in1=second[:, places], op=MAX)
+
+        hid_codes = [sbuf("hid_codes%d" % h, [P, HALF], U32) for h in range(2)]
+        hid_bytes = [sbuf("hid_bytes%d" % h, [P, HALF], U8) for h in range(2)]
+        for h in range(2):
+            nc.vector.quantize_mx(
+                out=hid_codes[h][:].bitcast(FP8X4), scales=hid_bytes[h][:], in_=hid_woven[h][:].rearrange("p o t -> p (o t)")
+            )
+
+        def second_product(bank, b, h):
+            rows = slice(b * P, (b + 1) * P)
             nc.tensor.matmul_mx(
-                out=bank[:],
+                out=bank,
                 lhsT=vs_codes[:, rows].bitcast(FP8X4),
                 lhsT_scale=vs_bytes[:, rows],
-                rhs=hid_codes[:].bitcast(FP8X4),
-                rhs_scale=hid_bytes[:],
+                rhs=hid_codes[h][:].bitcast(FP8X4),
+                rhs_scale=hid_bytes[h][:],
                 start=True,
                 stop=True,
             )
-            if half == 0:
-                nc.scalar.copy(out=result[:], in_=bank[:])
-                nc.scalar.dma_start(out[rows, :], result[:])
+
+        out_blocks = out.rearrange("(b p) o -> p b o", p=P)
+        left_bank = psum.tile([P, 2, HALF], F32, name="left_bank")
+        left = sbuf("left", [P, 2, HALF], F32)
+        for b in range(2):
+            second_product(left_bank[:, b, :], b, 0)
+        nc.scalar.copy(out=left[:], in_=left_bank[:])
+        nc.sync.dma_start(out_blocks[:, :, 0:HALF], left[:])
+        for b in range(2):
+            bank = psum.tile([P, HALF], F32, name="right_bank%d" % b)
+            right = sbuf("right%d" % b, [P, HALF], F32)
+            second_product(bank[:], b, 1)
+            if b == 0:
+                nc.vector.tensor_copy(out=right[:], in_=bank[:])
+                nc.sync.dma_start(out_blocks[:, b, HALF:O], right[:])
             else:
-                nc.vector.tensor_copy(out=result[:], in_=bank[:])
-                nc.sync.dma_start(out[rows, :], result[:])
+                nc.scalar.copy(out=right[:], in_=bank[:])
+                nc.scalar.dma_start(out_blocks[:, b, HALF:O], right[:])

from contextlib import ExitStack

import concourse.mybir as mybir

K, J, R, T, F, G, O, C, N, S = 512, 512, 512, 1024, 1024, 384, 256, 1024, 256, 1024
FLOPS = 2 * K * R * J + 2 * R * N * O

F32 = mybir.dt.float32
BF16 = mybir.dt.bfloat16
I32 = mybir.dt.int32
U32 = mybir.dt.uint32
U16 = mybir.dt.uint16
U8 = mybir.dt.uint8
FP8X4 = mybir.dt.float8_e4m3fn_x4
COPY = mybir.ActivationFunctionType.Copy
MAX = mybir.AluOpType.max

P = 128
PACK = 4
FIRST = 128
HALF = O // 2


def tile_picked_tokens_sparsecodes_one_boardpair_store_plain_kernel(
    tc, xt_words, xt_scales, ua, ha, sa, sb, vs_words, vs_scales, offs, offs2, offs3, offs4, offs5, offs6, offs7, out
):
    nc = tc.nc
    with ExitStack() as ctx:
        keep = ctx.enter_context(tc.tile_pool(name="keep", bufs=1))
        reused = ctx.enter_context(tc.tile_pool(name="reused", bufs=1))
        psum = ctx.enter_context(tc.psum_pool(name="psum", bufs=1))

        def sbuf(name, shape, dtype, tag=None):
            return keep.tile(shape, dtype, name=name, tag=tag or name, align_bytes=64)

        def load_list(name, source):
            tile = sbuf(name, list(source.shape), U16)
            nc.sync.dma_start(tile[:], source)
            return tile

        def load_words(tile, source):
            nc.sync.dma_start(tile[:], source[0].rearrange("p c t -> p (c t)").bitcast(I32))
            return tile

        def load_scale_rows(tile, source):
            for q in range(4):
                nc.sync.dma_start(tile[32 * q : 32 * q + 4, :].bitcast(I32), source[0, 4 * q : 4 * q + 4, :].bitcast(I32))

        def load_factor(name, source, engine):
            tile = sbuf(name, [P, PACK], F32)
            engine.dma_start(tile[:], source.rearrange("(p t) one -> p (t one)", t=PACK))
            return tile

        xt_scale_table = sbuf("xt_scale_table", [P, T], U8)
        vs_scale_table = sbuf("vs_scale_table", [P, S], U8)
        wc = {t: sbuf("wc%d" % t, [P, R], F32) for t in (0, 3)}
        board = [sbuf("board%d" % t, [P, C], F32) for t in range(PACK)]
        warm = sbuf("warm", [P, 16], F32)
        nc.vector.memset(warm[:, 0:8], 0.0)
        nc.scalar.activation(out=warm[:, 8:9], in_=warm[:, 0:1], func=COPY)
        nc.vector.memset(xt_scale_table[:].bitcast(I32), 0)
        nc.vector.memset(vs_scale_table[:].bitcast(I32), 0)
        for t in wc:
            nc.vector.memset(wc[t][:], 0.0)

        ua_rows = ua.rearrange("(p t) f -> p t f", t=PACK)
        ua_table = [sbuf("ua_table%d" % t, [P, F], F32) for t in range(PACK)]
        nc.sync.dma_start(ua_table[0][:], ua_rows[:, 0, :])
        step = load_factor("step", ha, nc.scalar)
        code_list = load_list("code_list", offs2)
        fill_list = load_list("fill_list", offs3)
        nc.sync.dma_start(ua_table[1][:], ua_rows[:, 1, :])
        nc.sync.dma_start(ua_table[2][:], ua_rows[:, 2, :])
        nc.sync.dma_start(ua_table[3][:], ua_rows[:, 3, :])
        store_list = load_list("store_list", offs7)
        load_scale_rows(vs_scale_table, vs_scales)
        vs_word_table = load_words(sbuf("vs_word_table", [P, S], I32), vs_words)
        token_list = load_list("token_list", offs)
        load_scale_rows(xt_scale_table, xt_scales)
        xt_word_table = load_words(reused.tile([P, T], I32, name="xt_word_table", align_bytes=64, offset=0), xt_words)
        put_list = load_list("put_list", offs4)
        first_list = load_list("first_list", offs5)
        second_list = load_list("second_list", offs6)

        for t in range(PACK):
            nc.vector.memset(board[t][:], 0.0)

        xt_codes = sbuf("xt_codes", [P, J], U32)
        xt_bytes = sbuf("xt_bytes", [P, J], U8)
        vs_codes = sbuf("vs_codes", [P, N], U32)
        vs_bytes = sbuf("vs_bytes", [P, N], U8)

        nc.vector.tensor_copy(out=vs_bytes[:], in_=vs_scale_table[:].indirect(store_list[:]))
        nc.vector.tensor_copy(out=vs_codes[:], in_=vs_word_table[:].bitcast(U32).indirect(store_list[:]))
        nc.vector.tensor_copy(out=xt_bytes[:], in_=xt_scale_table[:].indirect(token_list[:]))
        nc.vector.tensor_copy(out=xt_codes[:], in_=xt_word_table[:].bitcast(U32).indirect(token_list[:]))

        wc_codes = [sbuf("wc_codes%d" % u, [P, P], U32) for u in range(PACK)]
        wc_bytes = [sbuf("wc_bytes%d" % u, [P, P], U8) for u in range(PACK)]
        woven_tags = [0, 1]

        def woven_tile(u):
            if u < 2:
                return reused.tile([P, P, PACK], BF16, name="wc_woven%d" % u, align_bytes=64, offset=u * 1024)
            return sbuf("wc_woven%d" % u, [P, P, PACK], BF16, tag="wc_codes%d" % (u - 1))

        def weave_wc(woven, t, u):
            nc.vector.tensor_copy(out=woven[:, :, t], in_=wc[t][:].rearrange("p (m u) -> p m u", u=PACK)[:, :, u])

        early = [woven_tile(u) for u in range(len(woven_tags))]
        for t in range(PACK):
            wcd = sbuf("wcd%d" % t, [P, G], F32)
            nc.scalar.activation(out=wcd[:], in_=ua_table[t][:].indirect(code_list[:]), func=COPY, scale=step[:, t : t + 1])
            if t not in wc:
                wc[t] = sbuf("wc%d" % t, [P, R], F32, tag="ua_table%d" % t)
                nc.vector.memset(wc[t][:], 0.0)
            nc.scalar.activation(out=wc[t][:].indirect(fill_list[:]), in_=wcd[:], func=COPY)
            if t < PACK - 1:
                for u, woven in enumerate(early):
                    weave_wc(woven, t, u)

        def first_product(u, bank, bank_col, j0, j1):
            nc.tensor.matmul_mx(
                out=bank[:, bank_col : bank_col + j1 - j0],
                lhsT=wc_codes[u][:].bitcast(FP8X4),
                lhsT_scale=wc_bytes[u][:],
                rhs=xt_codes[:, j0:j1].bitcast(FP8X4),
                rhs_scale=xt_bytes[:, j0:j1],
                start=True,
                stop=True,
            )

        def put(u, values, j0, j1):
            nc.scalar.activation(out=board[u][:].indirect(put_list[:, j0 // 16 : j1 // 16]), in_=values, func=COPY)

        pairs = []

        def read_board(u):
            first = sbuf("first%d" % u, [P, O], F32)
            second = sbuf("second%d" % u, [P, O], F32)
            nc.scalar.activation(out=first[:], in_=board[u][:].indirect(first_list[:]), func=COPY, scale=first_weight[:, u : u + 1])
            nc.scalar.activation(out=second[:], in_=board[u][:].indirect(second_list[:]), func=COPY, scale=second_weight[:, u : u + 1])
            pairs.append((first, second))

        for u in range(PACK):
            if u < len(early):
                woven = early[u]
                weave_wc(woven, PACK - 1, u)
            else:
                woven = woven_tile(u)
                for t in range(PACK):
                    weave_wc(woven, t, u)
            nc.vector.quantize_mx(
                out=wc_codes[u][:].bitcast(FP8X4), scales=wc_bytes[u][:], in_=woven[:].rearrange("p m t -> p (m t)")
            )
            if u == 0:
                head_bank = psum.tile([P, FIRST], F32, name="head_bank")
                rest_bank = psum.tile([P, J - FIRST], F32, name="rest_bank")
                head = sbuf("a_head", [P, FIRST], F32)
                rest = sbuf("a_rest", [P, J - FIRST], F32)
                first_product(0, head_bank, 0, 0, FIRST)
                first_product(0, rest_bank, 0, FIRST, 2 * FIRST)
                first_product(0, rest_bank, FIRST, 2 * FIRST, J)
                nc.scalar.copy(out=head[:], in_=head_bank[:])
                nc.vector.tensor_copy(out=rest[:], in_=rest_bank[:])
                put(0, head[:], 0, FIRST)
                put(0, rest[:], FIRST, J)
            else:
                bank = psum.tile([P, J], F32, name="a_bank%d" % u)
                hidden = sbuf("a%d" % u, [P, J], F32)
                first_product(u, bank, 0, 0, J)
                nc.vector.tensor_copy(out=hidden[:], in_=bank[:])
                put(u, hidden[:], 0, J)

        weights = sbuf("weights", [P, 2, 2 * PACK], F32, tag="wc_bytes1")
        first_weight = weights[:, 0, :]
        second_weight = weights[:, 1, :]
        nc.sync.dma_start(first_weight[:, 0:PACK], sa.rearrange("(p t) one -> p (t one)", t=PACK))
        nc.sync.dma_start(second_weight[:, 0:PACK], sb.rearrange("(p t) one -> p (t one)", t=PACK))
        for u in range(PACK):
            read_board(u)

        hid_woven = [sbuf("hid_woven%d" % h, [P, HALF, PACK], BF16, tag=["wc_codes3", "wc_bytes3"][h]) for h in range(2)]
        for u, (first, second) in enumerate(pairs):
            for h in range(2):
                places = slice(h * HALF, (h + 1) * HALF)
                nc.vector.tensor_tensor(out=hid_woven[h][:, :, u], in0=first[:, places], in1=second[:, places], op=MAX)

        hid_codes = [sbuf("hid_codes%d" % h, [P, HALF], U32) for h in range(2)]
        hid_bytes = [sbuf("hid_bytes%d" % h, [P, HALF], U8) for h in range(2)]
        for h in range(2):
            nc.vector.quantize_mx(
                out=hid_codes[h][:].bitcast(FP8X4), scales=hid_bytes[h][:], in_=hid_woven[h][:].rearrange("p o t -> p (o t)")
            )

        def second_product(bank, b, h):
            rows = slice(b * P, (b + 1) * P)
            nc.tensor.matmul_mx(
                out=bank,
                lhsT=vs_codes[:, rows].bitcast(FP8X4),
                lhsT_scale=vs_bytes[:, rows],
                rhs=hid_codes[h][:].bitcast(FP8X4),
                rhs_scale=hid_bytes[h][:],
                start=True,
                stop=True,
            )

        out_blocks = out.rearrange("(b p) o -> p b o", p=P)
        left_bank = psum.tile([P, 2, HALF], F32, name="left_bank")
        left = sbuf("left", [P, 2, HALF], F32)
        for b in range(2):
            second_product(left_bank[:, b, :], b, 0)
        nc.scalar.copy(out=left[:], in_=left_bank[:])
        nc.sync.dma_start(out_blocks[:, :, 0:HALF], left[:])
        for b in range(2):
            bank = psum.tile([P, HALF], F32, name="right_bank%d" % b)
            right = sbuf("right%d" % b, [P, HALF], F32)
            second_product(bank[:], b, 1)
            if b == 0:
                nc.vector.tensor_copy(out=right[:], in_=bank[:])
                nc.sync.dma_start(out_blocks[:, b, HALF:O], right[:])
            else:
                nc.scalar.copy(out=right[:], in_=bank[:])
                nc.scalar.dma_start(out_blocks[:, b, HALF:O], right[:])
